import numpy as np, ml_dtypes
CORES = [0,1,2,3]
N = 4
PERM = [[0,3],[1,2],[2,1],[3,0]]
def setup_inputs(rng):
    return {"x": rng.standard_normal((N, 128, 8192), dtype=np.float32).astype(ml_dtypes.bfloat16)}
def reference(x):
    y = np.empty_like(x)
    for s, d in PERM:
        y[d] = x[s]
    return {"y": y}

SCRATCH = {
    "stage": ("sbuf", [128, 8192], "bfloat16"),
    "land": ("sbuf", [128, 8192], "bfloat16"),
}
SEMAPHORES = ["loaded", "read", "arrived", "stored"]

ENGINES = 16


def rank_program(g, core, T, topo):
    rank = T.rank_of(core)
    if rank is None:
        return

    perm = T.tables["PERM"]
    dst_rank = [d for s, d in perm if s == rank]
    src_rank = [s for s, d in perm if d == rank]

    sends = bool(dst_rank)
    receives = bool(src_rank)
    to_self = sends and dst_rank[0] == rank

    if sends:
        g.dma_start(T.stage[:], T.x[:]).then_inc(T.sem.loaded, 16)
        g.wait_ge(T.sem.loaded, 16)

    if to_self:
        g.dma_start(T.y[:], T.stage[:]).then_inc(T.sem.stored, 16)
        g.wait_ge(T.sem.stored, 16)
        return

    if sends:
        dst = T.cores[dst_rank[0]]
        rid, pid = topo.addr(dst)[:2]
        g.remote_dma(T.land[:], T.stage[:], T.sem.arrived, T.sem.read, pid, rid, topo.mask(core, dst))

    if receives:
        g.wait_ge(T.sem.arrived, ENGINES)
        g.dma_start(T.y[:], T.land[:]).then_inc(T.sem.stored, 16)
        g.wait_ge(T.sem.stored, 16)

    if sends:
        g.wait_ge(T.sem.read, ENGINES)
